import numpy as np
import ml_dtypes


def mxq(x, axis, fmt="e4m3"):
    dtype, down = {"e4m3": (ml_dtypes.float8_e4m3fn, 7), "e5m2": (ml_dtypes.float8_e5m2, 14)}[fmt]
    v = np.moveaxis(np.asarray(x, np.float32).astype(ml_dtypes.bfloat16).astype(np.float64), axis, -1)
    blocks = v.reshape(v.shape[:-1] + (-1, 32))
    amax = np.abs(blocks).max(-1, keepdims=True)
    byte = np.maximum(np.where(amax > 0, np.frexp(amax)[1] - 1 + 127, 0) - down, 1)
    scale = np.exp2(byte - 127.0)
    codes = (blocks / scale).astype(np.float32).astype(dtype).astype(np.float64)
    return np.moveaxis((codes * scale).reshape(v.shape), -1, axis)


WIDE = False


def mx_kscale(k):
    if not WIDE:
        return np.ones(k)
    levels = np.array([30, -30])
    if k % 512:
        return np.exp2(np.random.permutation(np.resize(levels, k // 32))).repeat(32)
    a = np.empty((k // 512, 16))
    for p in range(k // 512):
        a[p, :8] = np.random.permutation(np.resize(levels, 8))
        for g in range(8):
            far = levels[np.abs(levels - a[p, g]) >= 10]
            a[p, g + 8] = far[np.random.randint(len(far))]
    return np.exp2(a.ravel()).repeat(32)


def f64(x):
    return np.asarray(x).astype(np.float64)


def striped(idx):
    return np.tile(np.asarray(idx).reshape(-1, 16).T, (8, 1)).astype(np.uint16)


def unstriped(offs):
    return offs[:16].T.reshape(-1).astype(np.int64)


E2M1 = np.array([0.0, 0.5, 1.0, 1.5, 2.0, 3.0, 4.0, 6.0, -0.0, -0.5, -1.0, -1.5, -2.0, -3.0, -4.0, -6.0])


def pack_weight(w, fmt):
    k, n = w.shape
    w = f64(np.asarray(w, np.float32).astype(ml_dtypes.bfloat16)).reshape(k // 32, 32, n)
    amax = np.abs(w).max(1)
    if fmt in ("e4m3", "e5m2"):
        byte = np.frexp(amax)[1] - 1 + 127 - (7 if fmt == "e4m3" else 14)
    else:
        mant, ex = np.frexp(amax / 6.0)
        byte = np.where(mant > 0.5, ex, ex - 1) + 127
    byte = np.clip(np.where(amax > 0, byte, 1), 1, 254)
    scaled = (w * np.exp2(127.0 - byte)[:, None, :]).reshape(k, n).astype(np.float32)
    by_word = np.ascontiguousarray(scaled.reshape(k // 512, 128, 4, n).transpose(0, 1, 3, 2))
    if fmt in ("e4m3", "e5m2"):
        words = by_word.astype(ml_dtypes.float8_e4m3fn if fmt == "e4m3" else ml_dtypes.float8_e5m2).view(np.uint8)
    else:
        c = by_word.astype(ml_dtypes.float4_e2m1fn).view(np.uint8) & 0xF
        words = (c[..., 0::2] | (c[..., 1::2] << 4)).reshape(k // 512, 128, 2 * n)
    return np.ascontiguousarray(words), np.ascontiguousarray(byte.astype(np.uint8).reshape(k // 512, 16, n))


def unpack_weight(words, scales, fmt):
    g, _, n = scales.shape
    words = np.ascontiguousarray(words).reshape(g, 128, n, -1)
    if fmt in ("e4m3", "e5m2"):
        vals = words.view(ml_dtypes.float8_e4m3fn if fmt == "e4m3" else ml_dtypes.float8_e5m2).astype(np.float64)
    else:
        nib = np.empty((g, 128, n, 4), np.uint8)
        nib[..., 0::2] = words & 0xF
        nib[..., 1::2] = words >> 4
        vals = E2M1[nib]
    vals = vals * np.repeat(np.exp2(scales.astype(np.float64) - 127.0), 8, axis=1)[..., None]
    return vals.transpose(0, 1, 3, 2).reshape(g * 512, n)


K, T, J, R, F, Z, I, O, N, S = 512, 1024, 256, 512, 512, 1024, 256, 128, 256, 1024


def setup_inputs():
    n = np.random.standard_normal
    idx = np.random.permutation(T)[:J]
    idx2 = np.random.permutation(Z)[:J]
    idx3 = np.random.permutation(J)[:I]
    idx4 = np.random.permutation(J)[:I]
    idx5 = np.random.permutation(I)[:O]
    idx6 = np.random.permutation(I)[:O]
    idx7 = np.random.permutation(S)[:N]
    fk = mx_kscale(K)
    ff = mx_kscale(F)
    fr = mx_kscale(R)
    xtp = pack_weight(n((K, T)) / fk[:, None], "e5m2")
    xop = pack_weight(n((F, Z)) / ff[:, None], "e4m3")
    wp = pack_weight(n((K, R)) * 1 / np.sqrt(K) * fk[:, None] * fr, "e2m1")
    w2p = pack_weight(n((F, R)) * 1 / np.sqrt(F) * ff[:, None], "e2m1")
    vsp = pack_weight(n((R, S)) * 1 / np.sqrt(R) / fr[:, None], "e2m1")
    return {
        "xt_words": xtp[0],
        "xt_scales": xtp[1],
        "xo_words": xop[0],
        "xo_scales": xop[1],
        "w_words": wp[0],
        "w_scales": wp[1],
        "w2_words": w2p[0],
        "w2_scales": w2p[1],
        "vs_words": vsp[0],
        "vs_scales": vsp[1],
        "offs": striped(idx),
        "offs2": striped(idx2),
        "offs3": striped(idx3),
        "offs4": striped(idx4),
        "offs5": striped(idx5),
        "offs6": striped(idx6),
        "offs7": striped(idx7),
    }


def reference(xt_words, xt_scales, xo_words, xo_scales, w_words, w_scales, w2_words, w2_scales, vs_words, vs_scales, offs, offs2, offs3, offs4, offs5, offs6, offs7):
    idx = unstriped(offs)
    idx2 = unstriped(offs2)
    idx3 = unstriped(offs3)
    idx4 = unstriped(offs4)
    idx5 = unstriped(offs5)
    idx6 = unstriped(offs6)
    idx7 = unstriped(offs7)
    xtu = unpack_weight(xt_words, xt_scales, "e5m2")
    xou = unpack_weight(xo_words, xo_scales, "e4m3")
    wu = unpack_weight(w_words, w_scales, "e2m1")
    w2u = unpack_weight(w2_words, w2_scales, "e2m1")
    vsu = unpack_weight(vs_words, vs_scales, "e2m1")
    xtidxg = xtu[:, idx]
    a = wu.T @ xtidxg
    xoidx2g = xou[:, idx2]
    b = w2u.T @ xoidx2g
    lb = b[:, 0:1]
    la = a[:, 0:1]
    h1 = np.maximum(a[:, idx3] * lb, b[:, idx4] * la)
    hid = np.abs(h1[:, idx5] - h1[:, idx6])
    vsidx7g = vsu[:, idx7]
    hidq = mxq(hid, 0, "e4m3")
    y = vsidx7g.T @ hidq
    return y

@@ -1,0 +1,155 @@
+from contextlib import ExitStack
+
+import concourse.mybir as mybir
+
+K, T, J, R, F, Z, I, O, N, S = 512, 1024, 256, 512, 512, 1024, 256, 128, 256, 1024
+FLOPS = 2 * (K * R * J + F * R * J + R * N * O)
+
+F32 = mybir.dt.float32
+BF16 = mybir.dt.bfloat16
+I32 = mybir.dt.int32
+U32 = mybir.dt.uint32
+U16 = mybir.dt.uint16
+U8 = mybir.dt.uint8
+E4M3 = mybir.dt.float8_e4m3fn_x4
+E5M2 = mybir.dt.float8_e5m2_x4
+E2M1 = mybir.dt.float4_e2m1fn_x4
+ACT = mybir.ActivationFunctionType
+ALU = mybir.AluOpType
+
+P = 128
+PACK = 4
+QUADS = 4
+
+
+def tile_list_leadmeetthenlook_twotab_store_plain_kernel(
+    tc, xt_words, xt_scales, xo_words, xo_scales, w_words, w_scales, w2_words, w2_scales,
+    vs_words, vs_scales, offs, offs2, offs3, offs4, offs5, offs6, offs7, out,
+):
+    nc = tc.nc
+    with ExitStack() as ctx:
+        sb = ctx.enter_context(tc.tile_pool(name="sb", bufs=1))
+        ps = ctx.enter_context(tc.psum_pool(name="ps", bufs=1))
+
+        def new(name, shape, dtype):
+            return sb.tile(shape, dtype, name=name, align_bytes=64)
+
+        def load_list(name, src):
+            tile = new(name, list(src.shape), U16)
+            nc.sync.dma_start(tile[:], src)
+            return tile
+
+        def load_scale_rows(queue, tile, src):
+            rows = src[0].bitcast(I32)
+            for q in range(QUADS):
+                queue.dma_start(tile[32 * q : 32 * q + 4, :].bitcast(I32), rows[4 * q : 4 * q + 4, :])
+
+        xt_sc = new("xt_sc", [P, T], U8)
+        xo_sc = new("xo_sc", [P, Z], U8)
+        vs_sc = new("vs_sc", [P, S], U8)
+        ww_sc = new("ww_sc", [P, 2 * R], U8)
+        nc.vector.memset(xt_sc[:].bitcast(I32), 0)
+        nc.vector.memset(xo_sc[:].bitcast(I32), 0)
+        nc.vector.memset(ww_sc[:].bitcast(I32), 0)
+        nc.gpsimd.memset(vs_sc[:].bitcast(I32), 0)
+
+        xt_w = new("xt_w", [P, T], U32)
+        xo_w = new("xo_w", [P, Z], U32)
+        w_w = new("w_w", [P, R], U16)
+        w2_w = new("w2_w", [P, R], U16)
+        vs_w = new("vs_w", [P, S], U16)
+        ww_stage = new("ww_stage", [4, QUADS, 2, R // 4], I32)
+
+        nc.scalar.dma_start(xt_w[:].bitcast(I32), xt_words[0].rearrange("p n t -> p (n t)").bitcast(I32))
+        nc.sync.dma_start(ww_stage[:, :, 0, :], w_scales[0].bitcast(I32).rearrange("(q r) c -> r q c", r=4))
+        nc.sync.dma_start(ww_stage[:, :, 1, :], w2_scales[0].bitcast(I32).rearrange("(q r) c -> r q c", r=4))
+        l1 = load_list("l1", offs)
+        load_scale_rows(nc.sync, xt_sc, xt_scales)
+        nc.sync.dma_start(w_w[:].bitcast(I32), w_words[0].bitcast(I32))
+        nc.sync.dma_start(xo_w[:].bitcast(I32), xo_words[0].rearrange("p n t -> p (n t)").bitcast(I32))
+        l2 = load_list("l2", offs2)
+        load_scale_rows(nc.sync, xo_sc, xo_scales)
+        nc.sync.dma_start(w2_w[:].bitcast(I32), w2_words[0].bitcast(I32))
+        l3 = load_list("l3", offs3)
+        l4 = load_list("l4", offs4)
+        l7 = load_list("l7", offs7)
+        nc.sync.dma_start(vs_w[:].bitcast(I32), vs_words[0].bitcast(I32))
+        l5 = load_list("l5", offs5)
+        l6 = load_list("l6", offs6)
+        load_scale_rows(nc.gpsimd, vs_sc, vs_scales)
+
+        for q in range(QUADS):
+            nc.vector.tensor_copy(
+                ww_sc[32 * q : 32 * q + 4, :].bitcast(I32),
+                ww_stage[:, q, :, :].rearrange("r m c -> r (m c)"),
+            )
+        ww_dealt = new("ww_dealt", [P, 2, PACK, P], U8)
+        nc.vector.tensor_copy(ww_dealt[:], ww_sc[:].rearrange("p (m c t) -> p m t c", m=2, t=PACK))
+
+        w_dealt = new("w_dealt", [P, PACK, P], U16)
+        w2_dealt = new("w2_dealt", [P, PACK, P], U16)
+        nc.scalar.copy(w_dealt[:], w_w[:].rearrange("p (c t) -> p t c", t=PACK))
+        nc.scalar.copy(w2_dealt[:], w2_w[:].rearrange("p (c t) -> p t c", t=PACK))
+
+        def gather(name, window, offsets, width, dtype):
+            tile = new(name, [P, width], dtype)
+            nc.vector.tensor_copy(tile[:], window[:].indirect(offsets[:]))
+            return tile
+
+        xt_scg = gather("xt_scg", xt_sc, l1, J, U8)
+        xt_wg = gather("xt_wg", xt_w, l1, J, U32)
+        a_ps = [ps.tile([P, 2, J], F32, name=f"a_ps{h}") for h in range(2)]
+        for t in range(PACK):
+            nc.tensor.matmul_mx(
+                a_ps[t // 2][:, t % 2, :], lhsT=w_dealt[:, t, :].bitcast(E2M1), lhsT_scale=ww_dealt[:, 0, t, :],
+                rhs=xt_wg[:].bitcast(E5M2), rhs_scale=xt_scg[:], start=True, stop=True)
+        xo_scg = gather("xo_scg", xo_sc, l2, J, U8)
+        xo_wg = gather("xo_wg", xo_w, l2, J, U32)
+        b_ps = [ps.tile([P, J], F32, name=f"b_ps{t}") for t in range(PACK)]
+        for t in range(PACK):
+            nc.tensor.matmul_mx(
+                b_ps[t][:], lhsT=w2_dealt[:, t, :].bitcast(E2M1), lhsT_scale=ww_dealt[:, 1, t, :],
+                rhs=xo_wg[:].bitcast(E4M3), rhs_scale=xo_scg[:], start=True, stop=True)
+
+        a_sb = [new(f"a_sb{t}", [P, 2 * J], F32) for t in range(PACK)]
+        b_sb = [new(f"b_sb{t}", [P, 2 * J], F32) for t in range(PACK)]
+        for t in range(PACK):
+            nc.scalar.copy(a_sb[t][:, 0:J], a_ps[t // 2][:, t % 2, :])
+        for t in range(PACK):
+            nc.vector.tensor_copy(b_sb[t][:, 0:J], b_ps[t][:])
+
+        diff = new("diff", [P, PACK, O], F32)
+        for t in range(PACK):
+            ga = new(f"ga{t}", [P, I], F32)
+            gb = new(f"gb{t}", [P, I], F32)
+            nc.scalar.activation(ga[:], a_sb[t][:].indirect(l3[:]), ACT.Copy, scale=b_sb[t][:, 0:1])
+            nc.scalar.activation(gb[:], b_sb[t][:].indirect(l4[:]), ACT.Copy, scale=a_sb[t][:, 0:1])
+            h1 = new(f"h1_{t}", [P, I], F32)
+            nc.vector.tensor_tensor(h1[:], ga[:], gb[:], ALU.max)
+            g5 = gather(f"g5_{t}", h1, l5, O, F32)
+            nc.vector.tensor_tensor(diff[:, t, :], h1[:].indirect(l6[:]), g5[:], ALU.subtract)
+            if t == 0:
+                vs_scg = gather("vs_scg", vs_sc, l7, N, U8)
+            if t == 1:
+                vs_wg = gather("vs_wg", vs_w, l7, N, U16)
+
+        hid = new("hid", [P, O, PACK], BF16)
+        nc.scalar.activation(
+            hid[:].rearrange("p (c i) t -> p c t i", i=4), diff[:].rearrange("p t (c i) -> p c t i", i=4), ACT.Abs)
+        hid_w = new("hid_w", [P, O], U32)
+        hid_sc = new("hid_sc", [P, O], U8)
+        nc.vector.quantize_mx(hid_w[:].bitcast(E4M3), hid_sc[:], hid[:].rearrange("p o t -> p (o t)"))
+
+        for h in range(N // P):
+            y_ps = ps.tile([P, O], F32, name=f"y_ps{h}")
+            cols = slice(h * P, (h + 1) * P)
+            nc.tensor.matmul_mx(
+                y_ps[:], lhsT=vs_wg[:, cols].bitcast(E2M1), lhsT_scale=vs_scg[:, cols],
+                rhs=hid_w[:].bitcast(E4M3), rhs_scale=hid_sc[:], start=True, stop=True)
+            y = new(f"y{h}", [P, O], F32)
+            if h == 0:
+                nc.vector.tensor_copy(y[:], y_ps[:])
+                nc.sync.dma_start(out[cols, :], y[:])
+            else:
+                nc.scalar.copy(y[:], y_ps[:])
+                nc.scalar.dma_start(out[cols, :], y[:])

@@ -31,8 +31,8 @@ def tile_list_leadmeetthenlook_twotab_store_plain_kernel(
         sb = ctx.enter_context(tc.tile_pool(name="sb", bufs=1))
         ps = ctx.enter_context(tc.psum_pool(name="ps", bufs=1))
 
-        def new(name, shape, dtype):
-            return sb.tile(shape, dtype, name=name, align_bytes=64)
+        def new(name, shape, dtype, tag=""):
+            return sb.tile(shape, dtype, name=name, tag=tag or name, align_bytes=64)
 
         def load_list(name, src):
             tile = new(name, list(src.shape), U16)
@@ -51,7 +51,7 @@ def tile_list_leadmeetthenlook_twotab_store_plain_kernel(
         nc.vector.memset(xt_sc[:].bitcast(I32), 0)
         nc.vector.memset(xo_sc[:].bitcast(I32), 0)
         nc.vector.memset(ww_sc[:].bitcast(I32), 0)
-        nc.gpsimd.memset(vs_sc[:].bitcast(I32), 0)
+        nc.vector.memset(vs_sc[:].bitcast(I32), 0)
 
         xt_w = new("xt_w", [P, T], U32)
         xo_w = new("xo_w", [P, Z], U32)
@@ -60,39 +60,42 @@ def tile_list_leadmeetthenlook_twotab_store_plain_kernel(
         vs_w = new("vs_w", [P, S], U16)
         ww_stage = new("ww_stage", [4, QUADS, 2, R // 4], I32)
 
-        nc.scalar.dma_start(xt_w[:].bitcast(I32), xt_words[0].rearrange("p n t -> p (n t)").bitcast(I32))
+        nc.gpsimd.dma_start(w_w[:].bitcast(I32), w_words[0].bitcast(I32))
+        nc.gpsimd.dma_start(w2_w[:].bitcast(I32), w2_words[0].bitcast(I32))
         nc.sync.dma_start(ww_stage[:, :, 0, :], w_scales[0].bitcast(I32).rearrange("(q r) c -> r q c", r=4))
         nc.sync.dma_start(ww_stage[:, :, 1, :], w2_scales[0].bitcast(I32).rearrange("(q r) c -> r q c", r=4))
         l1 = load_list("l1", offs)
+        nc.sync.dma_start(xt_w[:].bitcast(I32), xt_words[0].rearrange("p n t -> p (n t)").bitcast(I32))
         load_scale_rows(nc.sync, xt_sc, xt_scales)
-        nc.sync.dma_start(w_w[:].bitcast(I32), w_words[0].bitcast(I32))
         nc.sync.dma_start(xo_w[:].bitcast(I32), xo_words[0].rearrange("p n t -> p (n t)").bitcast(I32))
         l2 = load_list("l2", offs2)
         load_scale_rows(nc.sync, xo_sc, xo_scales)
-        nc.sync.dma_start(w2_w[:].bitcast(I32), w2_words[0].bitcast(I32))
-        l3 = load_list("l3", offs3)
-        l4 = load_list("l4", offs4)
         l7 = load_list("l7", offs7)
-        nc.sync.dma_start(vs_w[:].bitcast(I32), vs_words[0].bitcast(I32))
+        l3 = load_list("l3", offs3)
         l5 = load_list("l5", offs5)
         l6 = load_list("l6", offs6)
-        load_scale_rows(nc.gpsimd, vs_sc, vs_scales)
+        l4 = load_list("l4", offs4)
+        nc.gpsimd.dma_start(vs_w[:].bitcast(I32), vs_words[0].bitcast(I32))
+        load_scale_rows(nc.sync, vs_sc, vs_scales)
 
         for q in range(QUADS):
             nc.vector.tensor_copy(
                 ww_sc[32 * q : 32 * q + 4, :].bitcast(I32),
                 ww_stage[:, q, :, :].rearrange("r m c -> r (m c)"),
             )
-        ww_dealt = new("ww_dealt", [P, 2, PACK, P], U8)
-        nc.vector.tensor_copy(ww_dealt[:], ww_sc[:].rearrange("p (m c t) -> p m t c", m=2, t=PACK))
+        w_sc_dealt = new("w_sc_dealt", [P, PACK, P], U8)
+        w2_sc_dealt = new("w2_sc_dealt", [P, PACK, P], U8)
+        nc.vector.tensor_copy(w_sc_dealt[:], ww_sc[:, 0:R].rearrange("p (c t) -> p t c", t=PACK))
 
         w_dealt = new("w_dealt", [P, PACK, P], U16)
         w2_dealt = new("w2_dealt", [P, PACK, P], U16)
-        nc.scalar.copy(w_dealt[:], w_w[:].rearrange("p (c t) -> p t c", t=PACK))
+        w_view = w_w[:].rearrange("p (c t) -> p t c", t=PACK)
+        nc.scalar.copy(w_dealt[:, 0:2, :], w_view[:, 0:2, :])
+        nc.scalar.copy(w_dealt[:, 2:4, :], w_view[:, 2:4, :])
         nc.scalar.copy(w2_dealt[:], w2_w[:].rearrange("p (c t) -> p t c", t=PACK))
 
-        def gather(name, window, offsets, width, dtype):
-            tile = new(name, [P, width], dtype)
+        def gather(name, window, offsets, width, dtype, tag=""):
+            tile = new(name, [P, width], dtype, tag)
             nc.vector.tensor_copy(tile[:], window[:].indirect(offsets[:]))
             return tile
 
@@ -101,47 +104,84 @@ def tile_list_leadmeetthenlook_twotab_store_plain_kernel(
         a_ps = [ps.tile([P, 2, J], F32, name=f"a_ps{h}") for h in range(2)]
         for t in range(PACK):
             nc.tensor.matmul_mx(
-                a_ps[t // 2][:, t % 2, :], lhsT=w_dealt[:, t, :].bitcast(E2M1), lhsT_scale=ww_dealt[:, 0, t, :],
+                a_ps[t // 2][:, t % 2, :], lhsT=w_dealt[:, t, :].bitcast(E2M1), lhsT_scale=w_sc_dealt[:, t, :],
                 rhs=xt_wg[:].bitcast(E5M2), rhs_scale=xt_scg[:], start=True, stop=True)
-        xo_scg = gather("xo_scg", xo_sc, l2, J, U8)
-        xo_wg = gather("xo_wg", xo_w, l2, J, U32)
-        b_ps = [ps.tile([P, J], F32, name=f"b_ps{t}") for t in range(PACK)]
-        for t in range(PACK):
-            nc.tensor.matmul_mx(
-                b_ps[t][:], lhsT=w2_dealt[:, t, :].bitcast(E2M1), lhsT_scale=ww_dealt[:, 1, t, :],
-                rhs=xo_wg[:].bitcast(E4M3), rhs_scale=xo_scg[:], start=True, stop=True)
-
-        a_sb = [new(f"a_sb{t}", [P, 2 * J], F32) for t in range(PACK)]
+        a_sb = [new(f"a_sb{t}", [P, 2 * J], F32) for t in range(2)]
         b_sb = [new(f"b_sb{t}", [P, 2 * J], F32) for t in range(PACK)]
-        for t in range(PACK):
-            nc.scalar.copy(a_sb[t][:, 0:J], a_ps[t // 2][:, t % 2, :])
-        for t in range(PACK):
-            nc.vector.tensor_copy(b_sb[t][:, 0:J], b_ps[t][:])
+        for t in range(2):
+            nc.scalar.copy(a_sb[t][:, 0:J], a_ps[0][:, t, :])
+
+        xo_wg = new("xo_wg", [P, J], U32)
+        xo_scg = new("xo_scg", [P, J], U8)
+        w2_sc_view = ww_sc[:, R : 2 * R].rearrange("p (c t) -> p t c", t=PACK)
+        lo, hi, whole = slice(0, J // 2), slice(J // 2, J), slice(0, J)
+
+        def gather_notes(cols):
+            entries = l2[:, cols.start // 16 : cols.stop // 16]
+            nc.vector.tensor_copy(xo_wg[:, cols], xo_w[:].indirect(entries))
+            nc.vector.tensor_copy(xo_scg[:, cols], xo_sc[:].indirect(entries))
+
+        def product_b(t, cols, name):
+            bank = ps.tile([P, cols.stop - cols.start], F32, name=name)
+            nc.tensor.matmul_mx(
+                bank[:], lhsT=w2_dealt[:, t, :].bitcast(E2M1), lhsT_scale=w2_sc_dealt[:, t, :],
+                rhs=xo_wg[:, cols].bitcast(E4M3), rhs_scale=xo_scg[:, cols], start=True, stop=True)
+            return bank
+
+        nc.vector.tensor_copy(w2_sc_dealt[:, 0, :], w2_sc_view[:, 0, :])
+        gather_notes(lo)
+        nc.scalar.copy(b_sb[0][:, lo], product_b(0, lo, "b_lo")[:])
+        gather_notes(hi)
+        nc.vector.tensor_copy(w2_sc_dealt[:, 1:, :], w2_sc_view[:, 1:, :])
+        vs_wg = gather("vs_wg", vs_w, l7, N, U16, "xo_sc")
+        nc.vector.tensor_copy(b_sb[0][:, hi], product_b(0, hi, "b_hi")[:])
+        for t in range(1, PACK):
+            nc.vector.tensor_copy(b_sb[t][:, whole], product_b(t, whole, f"b_ps{t}")[:])
 
         diff = new("diff", [P, PACK, O], F32)
+        hid = new("hid", [P, O, PACK], BF16)
+
+        def magnitude(pair):
+            ts = slice(2 * pair, 2 * pair + 2)
+            nc.scalar.activation(hid[:, :, ts], diff[:, ts, :].rearrange("p t o -> p o t"), ACT.Abs)
+
+        last = PACK - 1
+        picked = []
+
+        def subtract(t):
+            h1, g5 = picked[t]
+            nc.vector.tensor_tensor(diff[:, t, :], h1[:].indirect(l6[:]), g5[:], ALU.subtract)
+
         for t in range(PACK):
-            ga = new(f"ga{t}", [P, I], F32)
+            ga = new(f"ga{t}", [P, I], F32, ["", "b_sb0", "a_sb0", "a_sb1"][t])
             gb = new(f"gb{t}", [P, I], F32)
             nc.scalar.activation(ga[:], a_sb[t][:].indirect(l3[:]), ACT.Copy, scale=b_sb[t][:, 0:1])
             nc.scalar.activation(gb[:], b_sb[t][:].indirect(l4[:]), ACT.Copy, scale=a_sb[t][:, 0:1])
-            h1 = new(f"h1_{t}", [P, I], F32)
+            h1 = new(f"h1_{t}", [P, I], F32, ["", "", "b_sb0", "a_sb0"][t])
             nc.vector.tensor_tensor(h1[:], ga[:], gb[:], ALU.max)
-            g5 = gather(f"g5_{t}", h1, l5, O, F32)
-            nc.vector.tensor_tensor(diff[:, t, :], h1[:].indirect(l6[:]), g5[:], ALU.subtract)
             if t == 0:
-                vs_scg = gather("vs_scg", vs_sc, l7, N, U8)
-            if t == 1:
-                vs_wg = gather("vs_wg", vs_w, l7, N, U16)
-
-        hid = new("hid", [P, O, PACK], BF16)
-        nc.scalar.activation(
-            hid[:].rearrange("p (c i) t -> p c t i", i=4), diff[:].rearrange("p t (c i) -> p c t i", i=4), ACT.Abs)
+                for u, tag in enumerate(["gb0", "ga0"]):
+                    a_sb.append(new(f"a_sb{2 + u}", [P, 2 * J], F32, tag))
+                    nc.vector.tensor_copy(a_sb[2 + u][:, 0:J], a_ps[1][:, u, :])
+            if t > 0:
+                subtract(t - 1)
+            if t < last:
+                g5 = gather(f"g5_{t}", h1, l5, O, F32)
+            else:
+                g5 = new(f"g5_{t}", [P, O], F32)
+                nc.scalar.activation(g5[:], h1[:].indirect(l5[:]), ACT.Copy)
+            picked.append((h1, g5))
+        g6 = gather("g6", h1, l6, O, F32)
+        magnitude(0)
+        nc.vector.tensor_tensor(diff[:, last, :], g6[:], g5[:], ALU.subtract)
+        magnitude(1)
+        vs_scg = gather("vs_scg", vs_sc, l7, N, U8, "a_sb0")
         hid_w = new("hid_w", [P, O], U32)
         hid_sc = new("hid_sc", [P, O], U8)
         nc.vector.quantize_mx(hid_w[:].bitcast(E4M3), hid_sc[:], hid[:].rearrange("p o t -> p (o t)"))
 
         for h in range(N // P):
-            y_ps = ps.tile([P, O], F32, name=f"y_ps{h}")
+            y_ps = ps.tile([P, O], F32, name=f"y_ps{h}", tag=f"a_ps{h}")
             cols = slice(h * P, (h + 1) * P)
             nc.tensor.matmul_mx(
                 y_ps[:], lhsT=vs_wg[:, cols].bitcast(E2M1), lhsT_scale=vs_scg[:, cols],

from contextlib import ExitStack

import concourse.mybir as mybir

K, T, J, R, F, Z, I, O, N, S = 512, 1024, 256, 512, 512, 1024, 256, 128, 256, 1024
FLOPS = 2 * (K * R * J + F * R * J + R * N * O)

F32 = mybir.dt.float32
BF16 = mybir.dt.bfloat16
I32 = mybir.dt.int32
U32 = mybir.dt.uint32
U16 = mybir.dt.uint16
U8 = mybir.dt.uint8
E4M3 = mybir.dt.float8_e4m3fn_x4
E5M2 = mybir.dt.float8_e5m2_x4
E2M1 = mybir.dt.float4_e2m1fn_x4
ACT = mybir.ActivationFunctionType
ALU = mybir.AluOpType

P = 128
PACK = 4
QUADS = 4


def tile_list_leadmeetthenlook_twotab_store_plain_kernel(
    tc, xt_words, xt_scales, xo_words, xo_scales, w_words, w_scales, w2_words, w2_scales,
    vs_words, vs_scales, offs, offs2, offs3, offs4, offs5, offs6, offs7, out,
):
    nc = tc.nc
    with ExitStack() as ctx:
        sb = ctx.enter_context(tc.tile_pool(name="sb", bufs=1))
        ps = ctx.enter_context(tc.psum_pool(name="ps", bufs=1))

        def new(name, shape, dtype, tag=""):
            return sb.tile(shape, dtype, name=name, tag=tag or name, align_bytes=64)

        def load_list(name, src):
            tile = new(name, list(src.shape), U16)
            nc.sync.dma_start(tile[:], src)
            return tile

        def load_scale_rows(queue, tile, src):
            rows = src[0].bitcast(I32)
            for q in range(QUADS):
                queue.dma_start(tile[32 * q : 32 * q + 4, :].bitcast(I32), rows[4 * q : 4 * q + 4, :])

        xt_sc = new("xt_sc", [P, T], U8)
        xo_sc = new("xo_sc", [P, Z], U8)
        vs_sc = new("vs_sc", [P, S], U8)
        ww_sc = new("ww_sc", [P, 2 * R], U8)
        nc.vector.memset(xt_sc[:].bitcast(I32), 0)
        nc.vector.memset(xo_sc[:].bitcast(I32), 0)
        nc.vector.memset(ww_sc[:].bitcast(I32), 0)
        nc.vector.memset(vs_sc[:].bitcast(I32), 0)

        xt_w = new("xt_w", [P, T], U32)
        xo_w = new("xo_w", [P, Z], U32)
        w_w = new("w_w", [P, R], U16)
        w2_w = new("w2_w", [P, R], U16)
        vs_w = new("vs_w", [P, S], U16)
        ww_stage = new("ww_stage", [4, QUADS, 2, R // 4], I32)

        nc.gpsimd.dma_start(w_w[:].bitcast(I32), w_words[0].bitcast(I32))
        nc.gpsimd.dma_start(w2_w[:].bitcast(I32), w2_words[0].bitcast(I32))
        nc.sync.dma_start(ww_stage[:, :, 0, :], w_scales[0].bitcast(I32).rearrange("(q r) c -> r q c", r=4))
        nc.sync.dma_start(ww_stage[:, :, 1, :], w2_scales[0].bitcast(I32).rearrange("(q r) c -> r q c", r=4))
        l1 = load_list("l1", offs)
        nc.sync.dma_start(xt_w[:].bitcast(I32), xt_words[0].rearrange("p n t -> p (n t)").bitcast(I32))
        load_scale_rows(nc.sync, xt_sc, xt_scales)
        nc.sync.dma_start(xo_w[:].bitcast(I32), xo_words[0].rearrange("p n t -> p (n t)").bitcast(I32))
        l2 = load_list("l2", offs2)
        load_scale_rows(nc.sync, xo_sc, xo_scales)
        l7 = load_list("l7", offs7)
        l3 = load_list("l3", offs3)
        l5 = load_list("l5", offs5)
        l6 = load_list("l6", offs6)
        l4 = load_list("l4", offs4)
        nc.gpsimd.dma_start(vs_w[:].bitcast(I32), vs_words[0].bitcast(I32))
        load_scale_rows(nc.sync, vs_sc, vs_scales)

        for q in range(QUADS):
            nc.vector.tensor_copy(
                ww_sc[32 * q : 32 * q + 4, :].bitcast(I32),
                ww_stage[:, q, :, :].rearrange("r m c -> r (m c)"),
            )
        w_sc_dealt = new("w_sc_dealt", [P, PACK, P], U8)
        w2_sc_dealt = new("w2_sc_dealt", [P, PACK, P], U8)
        nc.vector.tensor_copy(w_sc_dealt[:], ww_sc[:, 0:R].rearrange("p (c t) -> p t c", t=PACK))

        w_dealt = new("w_dealt", [P, PACK, P], U16)
        w2_dealt = new("w2_dealt", [P, PACK, P], U16)
        w_view = w_w[:].rearrange("p (c t) -> p t c", t=PACK)
        nc.scalar.copy(w_dealt[:, 0:2, :], w_view[:, 0:2, :])
        nc.scalar.copy(w_dealt[:, 2:4, :], w_view[:, 2:4, :])
        nc.scalar.copy(w2_dealt[:], w2_w[:].rearrange("p (c t) -> p t c", t=PACK))

        def gather(name, window, offsets, width, dtype, tag=""):
            tile = new(name, [P, width], dtype, tag)
            nc.vector.tensor_copy(tile[:], window[:].indirect(offsets[:]))
            return tile

        xt_scg = gather("xt_scg", xt_sc, l1, J, U8)
        xt_wg = gather("xt_wg", xt_w, l1, J, U32)
        a_ps = [ps.tile([P, 2, J], F32, name=f"a_ps{h}") for h in range(2)]
        for t in range(PACK):
            nc.tensor.matmul_mx(
                a_ps[t // 2][:, t % 2, :], lhsT=w_dealt[:, t, :].bitcast(E2M1), lhsT_scale=w_sc_dealt[:, t, :],
                rhs=xt_wg[:].bitcast(E5M2), rhs_scale=xt_scg[:], start=True, stop=True)
        a_sb = [new(f"a_sb{t}", [P, 2 * J], F32) for t in range(2)]
        b_sb = [new(f"b_sb{t}", [P, 2 * J], F32) for t in range(PACK)]
        for t in range(2):
            nc.scalar.copy(a_sb[t][:, 0:J], a_ps[0][:, t, :])

        xo_wg = new("xo_wg", [P, J], U32)
        xo_scg = new("xo_scg", [P, J], U8)
        w2_sc_view = ww_sc[:, R : 2 * R].rearrange("p (c t) -> p t c", t=PACK)
        lo, hi, whole = slice(0, J // 2), slice(J // 2, J), slice(0, J)

        def gather_notes(cols):
            entries = l2[:, cols.start // 16 : cols.stop // 16]
            nc.vector.tensor_copy(xo_wg[:, cols], xo_w[:].indirect(entries))
            nc.vector.tensor_copy(xo_scg[:, cols], xo_sc[:].indirect(entries))

        def product_b(t, cols, name):
            bank = ps.tile([P, cols.stop - cols.start], F32, name=name)
            nc.tensor.matmul_mx(
                bank[:], lhsT=w2_dealt[:, t, :].bitcast(E2M1), lhsT_scale=w2_sc_dealt[:, t, :],
                rhs=xo_wg[:, cols].bitcast(E4M3), rhs_scale=xo_scg[:, cols], start=True, stop=True)
            return bank

        nc.vector.tensor_copy(w2_sc_dealt[:, 0, :], w2_sc_view[:, 0, :])
        gather_notes(lo)
        nc.scalar.copy(b_sb[0][:, lo], product_b(0, lo, "b_lo")[:])
        gather_notes(hi)
        nc.vector.tensor_copy(w2_sc_dealt[:, 1:, :], w2_sc_view[:, 1:, :])
        vs_wg = gather("vs_wg", vs_w, l7, N, U16, "xo_sc")
        nc.vector.tensor_copy(b_sb[0][:, hi], product_b(0, hi, "b_hi")[:])
        for t in range(1, PACK):
            nc.vector.tensor_copy(b_sb[t][:, whole], product_b(t, whole, f"b_ps{t}")[:])

        diff = new("diff", [P, PACK, O], F32)
        hid = new("hid", [P, O, PACK], BF16)

        def magnitude(pair):
            ts = slice(2 * pair, 2 * pair + 2)
            nc.scalar.activation(hid[:, :, ts], diff[:, ts, :].rearrange("p t o -> p o t"), ACT.Abs)

        last = PACK - 1
        picked = []

        def subtract(t):
            h1, g5 = picked[t]
            nc.vector.tensor_tensor(diff[:, t, :], h1[:].indirect(l6[:]), g5[:], ALU.subtract)

        for t in range(PACK):
            ga = new(f"ga{t}", [P, I], F32, ["", "b_sb0", "a_sb0", "a_sb1"][t])
            gb = new(f"gb{t}", [P, I], F32)
            nc.scalar.activation(ga[:], a_sb[t][:].indirect(l3[:]), ACT.Copy, scale=b_sb[t][:, 0:1])
            nc.scalar.activation(gb[:], b_sb[t][:].indirect(l4[:]), ACT.Copy, scale=a_sb[t][:, 0:1])
            h1 = new(f"h1_{t}", [P, I], F32, ["", "", "b_sb0", "a_sb0"][t])
            nc.vector.tensor_tensor(h1[:], ga[:], gb[:], ALU.max)
            if t == 0:
                for u, tag in enumerate(["gb0", "ga0"]):
                    a_sb.append(new(f"a_sb{2 + u}", [P, 2 * J], F32, tag))
                    nc.vector.tensor_copy(a_sb[2 + u][:, 0:J], a_ps[1][:, u, :])
            if t > 0:
                subtract(t - 1)
            if t < last:
                g5 = gather(f"g5_{t}", h1, l5, O, F32)
            else:
                g5 = new(f"g5_{t}", [P, O], F32)
                nc.scalar.activation(g5[:], h1[:].indirect(l5[:]), ACT.Copy)
            picked.append((h1, g5))
        g6 = gather("g6", h1, l6, O, F32)
        magnitude(0)
        nc.vector.tensor_tensor(diff[:, last, :], g6[:], g5[:], ALU.subtract)
        magnitude(1)
        vs_scg = gather("vs_scg", vs_sc, l7, N, U8, "a_sb0")
        hid_w = new("hid_w", [P, O], U32)
        hid_sc = new("hid_sc", [P, O], U8)
        nc.vector.quantize_mx(hid_w[:].bitcast(E4M3), hid_sc[:], hid[:].rearrange("p o t -> p (o t)"))

        for h in range(N // P):
            y_ps = ps.tile([P, O], F32, name=f"y_ps{h}", tag=f"a_ps{h}")
            cols = slice(h * P, (h + 1) * P)
            nc.tensor.matmul_mx(
                y_ps[:], lhsT=vs_wg[:, cols].bitcast(E2M1), lhsT_scale=vs_scg[:, cols],
                rhs=hid_w[:].bitcast(E4M3), rhs_scale=hid_sc[:], start=True, stop=True)
            y = new(f"y{h}", [P, O], F32)
            if h == 0:
                nc.vector.tensor_copy(y[:], y_ps[:])
                nc.sync.dma_start(out[cols, :], y[:])
            else:
                nc.scalar.copy(y[:], y_ps[:])
                nc.scalar.dma_start(out[cols, :], y[:])
